import numpy as np
import ml_dtypes


def mxq(x, axis, fmt="e4m3"):
    dtype, down = {"e4m3": (ml_dtypes.float8_e4m3fn, 7), "e5m2": (ml_dtypes.float8_e5m2, 14)}[fmt]
    v = np.moveaxis(np.asarray(x, np.float32).astype(ml_dtypes.bfloat16).astype(np.float64), axis, -1)
    blocks = v.reshape(v.shape[:-1] + (-1, 32))
    amax = np.abs(blocks).max(-1, keepdims=True)
    byte = np.maximum(np.where(amax > 0, np.frexp(amax)[1] - 1 + 127, 0) - down, 1)
    scale = np.exp2(byte - 127.0)
    codes = (blocks / scale).astype(np.float32).astype(dtype).astype(np.float64)
    return np.moveaxis((codes * scale).reshape(v.shape), -1, axis)


WIDE = False


def mx_kscale(k):
    if not WIDE:
        return np.ones(k)
    levels = np.array([10, -10, 5, -5, 0])
    if k % 512:
        return np.exp2(np.random.permutation(np.resize(levels, k // 32))).repeat(32)
    a = np.empty((k // 512, 16))
    for p in range(k // 512):
        a[p, :8] = np.random.permutation(np.resize(levels, 8))
        for g in range(8):
            far = levels[np.abs(levels - a[p, g]) >= 10]
            a[p, g + 8] = far[np.random.randint(len(far))]
    return np.exp2(a.ravel()).repeat(32)


BF16 = ml_dtypes.bfloat16


def bf(x):
    return np.asarray(x, np.float32).astype(BF16)


def f64(x):
    return np.asarray(x).astype(np.float64)


E2M1 = np.array([0.0, 0.5, 1.0, 1.5, 2.0, 3.0, 4.0, 6.0, -0.0, -0.5, -1.0, -1.5, -2.0, -3.0, -4.0, -6.0])


def pack_weight(w, fmt):
    k, n = w.shape
    w = f64(bf(w)).reshape(k // 32, 32, n)
    amax = np.abs(w).max(1)
    if fmt == "e4m3":
        byte = np.frexp(amax)[1] - 1 + 127 - 7
    else:
        mant, ex = np.frexp(amax / 6.0)
        byte = np.where(mant > 0.5, ex, ex - 1) + 127
    byte = np.clip(np.where(amax > 0, byte, 1), 1, 254)
    scaled = (w * np.exp2(127.0 - byte)[:, None, :]).reshape(k, n).astype(np.float32)
    by_word = np.ascontiguousarray(scaled.reshape(k // 512, 128, 4, n).transpose(0, 1, 3, 2))
    if fmt == "e4m3":
        words = by_word.astype(ml_dtypes.float8_e4m3fn).view(np.uint8)
    else:
        c = by_word.astype(ml_dtypes.float4_e2m1fn).view(np.uint8) & 0xF
        words = c[..., 0::2] | (c[..., 1::2] << 4)
    return np.ascontiguousarray(words), np.ascontiguousarray(byte.astype(np.uint8).reshape(k // 512, 16, n))


def unpack_weight(words, scales, fmt):
    g, p, n, _ = words.shape
    if fmt == "e4m3":
        vals = np.ascontiguousarray(words).view(ml_dtypes.float8_e4m3fn).astype(np.float64)
    else:
        nib = np.empty((g, p, n, 4), np.uint8)
        nib[..., 0::2] = words & 0xF
        nib[..., 1::2] = words >> 4
        vals = E2M1[nib]
    vals = vals * np.repeat(np.exp2(scales.astype(np.float64) - 127.0), 8, axis=1)[..., None]
    return vals.transpose(0, 1, 3, 2).reshape(g * 512, n)
def pack4(w):
    words, scales = pack_weight(w, "e2m1")
    return words.reshape(words.shape[0], 128, -1), scales


def unpack4(words, scales):
    return unpack_weight(words.reshape(words.shape[0], 128, -1, 2), scales, "e2m1")


KD, KP, N = 512, 1024, 1536

FIELD_D, FIELD_P = 0.5, 0.25


def setup_inputs():
    s, t = mx_kscale(KD), mx_kscale(KP)
    spread = np.concatenate([FIELD_D * np.ones(KD), FIELD_P * np.ones(KP)])
    left = np.random.standard_normal((N, N)) * np.concatenate([s, t])
    r_d = np.random.standard_normal((KD, N)) / np.sqrt(KD) / s[:, None]
    r_p = np.random.standard_normal((KP, N)) / np.sqrt(KP) / t[:, None]
    r_p_words, r_p_scales = pack4(r_p)
    return {"left": bf(left),
            "f1": bf(np.random.standard_normal(N) * spread),
            "f2": bf(np.random.standard_normal(N) * spread),
            "r_d": bf(r_d),
            "r_p_words": r_p_words,
            "r_p_scales": r_p_scales}


def reference(left, f1, f2, r_d, r_p_words, r_p_scales):
    a = f64(left) * np.exp(f64(f1))
    a_d = mxq(a[:, :KD], 1, "e4m3")
    a_p = mxq(a[:, KD:], 1, "e4m3")
    w_d = mxq(f64(r_d), 0, "e4m3")
    w_p = unpack4(r_p_words, r_p_scales)
    pair = (a_d @ w_d) + (a_p @ w_p)
    return np.exp(f64(f2))[:, None] * pair

@@ -1,0 +1,279 @@
+from contextlib import ExitStack
+
+import concourse.mybir as mybir
+from concourse.masks import make_identity
+
+F32 = mybir.dt.float32
+BF16 = mybir.dt.bfloat16
+I32 = mybir.dt.int32
+U32 = mybir.dt.uint32
+U8 = mybir.dt.uint8
+FP8X4 = mybir.dt.float8_e4m3fn_x4
+FP4X4 = mybir.dt.float4_e2m1fn_x4
+MULT = mybir.AluOpType.mult
+ADD = mybir.AluOpType.add
+EXP = mybir.ActivationFunctionType.Exp
+COPY = mybir.ActivationFunctionType.Copy
+
+N = 1536
+FLOPS = 2 * N * N * N
+P = 128
+RT = N // P
+NPAIR = RT // 2
+NJ = 3
+JW = 512
+S_COLS = 320
+T_AT = {1: 2, 2: 3, 3: 0, 4: 1}
+PERM_AT = {(0, 1): ((2, 0), (2, 1)), (1, 3): ((3, 0),), (1, 5): ((3, 1),), (2, 1): ((4, 0),), (2, 3): ((4, 1),), (3, 1): ((5, 0),), (3, 3): ((5, 1),)}
+
+
+def tile_hubbard_slice_pair_s1_kernel(tc, left, f1, f2, r_d, r_p_words, r_p_scales, out):
+    nc = tc.nc
+    left_v = left.rearrange("(p i) c -> p i c", i=RT)
+    out_v = out.rearrange("(p i) n -> p i n", i=RT)
+    rd_v = r_d.rearrange("(p j) w -> p j w", j=4)
+    rpw_v = r_p_words.rearrange("g p n -> p g n")
+    rps_v = r_p_scales.rearrange("g q n -> q g n")
+
+    with ExitStack() as ctx:
+        keep = ctx.enter_context(tc.tile_pool(name="keep", bufs=1))
+        work = ctx.enter_context(tc.tile_pool(name="work", bufs=4))
+        psum = ctx.enter_context(tc.psum_pool(name="psum", bufs=8))
+        ctx.enter_context(tc.manual_schedule())
+
+        ident = keep.tile([P, P], F32, name="ident")
+        warm = keep.tile([P, 1], F32, name="warm")
+        f1_sb = keep.tile([P, 12], BF16, name="f1_sb")
+        f2_sb = keep.tile([P, 12], BF16, name="f2_sb")
+        ef1 = keep.tile([P, 12], F32, name="ef1")
+        ef2 = keep.tile([P, 12], F32, name="ef2")
+        rps = keep.tile([P, 2, N], U8, name="rps", align_bytes=64)
+        x_sb = [keep.tile([P, 2, N], BF16, name=f"x{k}", align_bytes=64) for k in range(NPAIR)]
+        rpw = [keep.tile([P, 2, 2 * JW], U8, name=f"rpw{j}", align_bytes=64) for j in range(NJ)]
+        rd_raw = [keep.tile([P, 4, JW], BF16, name=f"rdraw{j}", align_bytes=64) for j in range(NJ)]
+        rd_grp = [keep.tile([P, JW, 4], BF16, name=f"rdgrp{j}", align_bytes=64) for j in range(NJ)]
+        rdc = [keep.tile([P, JW], U32, name=f"rdc{j}", align_bytes=64) for j in range(NJ)]
+        rds = [keep.tile([P, JW], U8, name=f"rds{j}", align_bytes=64) for j in range(NJ)]
+        ac = [[keep.tile([P, 2 * P], U32, name=f"ac{k}_{g}", align_bytes=64) for g in range(3)] for k in range(NPAIR)]
+        asc = [[keep.tile([P, 2 * P], U8, name=f"as{k}_{g}", align_bytes=64) for g in range(3)] for k in range(NPAIR)]
+
+        nc.vector.memset(warm[:], 0.0)
+        nc.vector.memset(rps[:].rearrange("p g n -> p (g n)").bitcast(I32), 0)
+        make_identity(nc, ident[:])
+        nc.gpsimd.dma_start(out=f2_sb[:], in_=f2.rearrange("(p i) -> p i", i=RT))
+
+        nc.scalar.dma_start(out=f1_sb[:].rearrange("p (g t) -> p g t", t=4), in_=f1.rearrange("(g p t) -> p g t", p=P, t=4))
+        nc.scalar.activation(out=warm[:], in_=warm[:], func=EXP)
+
+        def load_x(k, u0, u1, c0, c1):
+            nc.sync.dma_start(out=x_sb[k][:, u0:u1, c0:c1], in_=left_v[:, 2 * k + u0 : 2 * k + u1, c0:c1])
+
+        def load_rpw(j):
+            nc.sync.dma_start(out=rpw[j][:].bitcast(I32), in_=rpw_v[:, :, 2 * JW * j : 2 * JW * (j + 1)].bitcast(I32))
+
+        def load_rd(j):
+            nc.sync.dma_start(out=rd_raw[j][:], in_=rd_v[:, :, JW * j : JW * (j + 1)])
+
+        load_x(0, 0, 1, 512, N)
+        load_x(0, 1, 2, 512, N)
+        load_rpw(0)
+        load_x(0, 0, 2, 0, 512)
+        for q in range(4):
+            nc.scalar.dma_start(out=rps[32 * q : 32 * q + 4, :, :].bitcast(I32), in_=rps_v[4 * q : 4 * q + 4, :, :].bitcast(I32))
+        load_rd(0)
+        load_rpw(1)
+        load_rd(1)
+        load_rd(2)
+        load_x(1, 0, 2, 512, N)
+        load_rpw(2)
+        load_x(1, 0, 2, 0, 512)
+        for k in range(2, NPAIR):
+            load_x(k, 0, 2, 0, N)
+
+        nc.scalar.activation(out=ef1[:], in_=f1_sb[:], func=EXP)
+        nc.scalar.activation(out=ef2[:], in_=f2_sb[:], func=EXP)
+
+        tbank = {}
+        words = {}
+
+        def perm(k, u):
+            if (k, "perm") not in words:
+                pt = work.tile([P, 2, 3, 2, P], F32, name="perm", tag="perm", bufs=2)
+                words[k, "perm"] = pt
+            pt = words[k, "perm"]
+            src = x_sb[k][:, u, :].bitcast(F32)
+            nc.scalar.copy(out=pt[:, u], in_=src.rearrange("p (g m v) -> p g v m", g=3, v=2))
+
+        def transpose(k, g, u):
+            if (k, g) not in tbank:
+                bank = psum.tile([P, JW], F32, name="bank", tag="bank")
+                tbank[k, g] = bank
+            for v in range(2):
+                if (k, "perm") in words:
+                    src = words[k, "perm"][:, u, g, v, :]
+                else:
+                    w = x_sb[k][:, u, :].bitcast(F32)
+                    src = w[:, 256 * g + v : 256 * (g + 1) : 2]
+                nc.tensor.transpose(tbank[k, g][:, 256 * v + P * u : 256 * v + P * (u + 1)], src, ident[:])
+
+        grp = {}
+
+        def scale_out(k, g, u0, u1):
+            if (k, g) not in grp:
+                gt = work.tile([P, 2 * P, 4], BF16, name="grp", tag="grp", align_bytes=64, bufs=6)
+                grp[k, g] = gt
+            n = P * (u1 - u0)
+            src = tbank[k, g][:].bitcast(BF16).rearrange("p (v x e) -> p x v e", v=2, e=2)[:, P * u0 : P * u1]
+            fac = ef1[:, 4 * g : 4 * g + 4].rearrange("p (v e) -> p v e", e=2).unsqueeze(1).to_broadcast([P, n, 2, 2])
+            dst = grp[k, g][:, P * u0 : P * u1, :].rearrange("p x (v e) -> p x v e", e=2)
+            nc.vector.tensor_tensor(out=dst, in0=src, in1=fac, op=MULT)
+
+        def quant(k, g, u0, u1):
+            nc.vector.quantize_mx(
+                out=ac[k][g][:, P * u0 : P * u1].bitcast(FP8X4),
+                scales=asc[k][g][:, P * u0 : P * u1],
+                in_=grp[k, g][:, P * u0 : P * u1, :].rearrange("p x t -> p (x t)"),
+            )
+
+        def interleave_rd(j):
+            nc.scalar.copy(out=rd_grp[j][:, :S_COLS, :], in_=rd_raw[j][:, :, :S_COLS].rearrange("p t w -> p w t"))
+            nc.gpsimd.tensor_scalar(
+                out=rd_grp[j][:, S_COLS:, :], in0=rd_raw[j][:, :, S_COLS:].rearrange("p t w -> p w t"),
+                scalar1=1.0, scalar2=0.0, op0=MULT, op1=ADD,
+            )
+
+        def quant_rd(j):
+            nc.vector.quantize_mx(out=rdc[j][:].bitcast(FP8X4), scales=rds[j][:], in_=rd_grp[j][:].rearrange("p w t -> p (w t)"))
+
+        acc = {}
+
+        def mm(k, u, j, g, start, stop):
+            if start:
+                bank = psum.tile([P, JW], F32, name="bank", tag="bank")
+                acc[k, u, j] = bank
+            if g == 0:
+                rhs = rdc[j][:].bitcast(FP8X4)
+                rhs_scale = rds[j][:]
+            else:
+                rhs = rpw[j][:, g - 1, :].bitcast(FP4X4)
+                rhs_scale = rps[:, g - 1, JW * j : JW * (j + 1)]
+            nc.tensor.matmul_mx(
+                out=acc[k, u, j][:],
+                lhsT=ac[k][g][:, P * u : P * (u + 1)].bitcast(FP8X4),
+                lhsT_scale=asc[k][g][:, P * u : P * (u + 1)],
+                rhs=rhs, rhs_scale=rhs_scale, start=start, stop=stop,
+            )
+
+        res = {}
+
+        def evac(k, u, j, engine="s"):
+            i = 2 * k + u
+            if i not in res:
+                rt = work.tile([P, N], F32, name="res", tag="res", bufs=4)
+                res[i] = rt
+            dst = res[i][:, JW * j : JW * (j + 1)]
+            if engine == "s":
+                nc.scalar.activation(out=dst, in_=acc[k, u, j][:], func=COPY, scale=ef2[:, i : i + 1])
+            else:
+                nc.vector.tensor_scalar(out=dst, in0=acc[k, u, j][:], scalar1=ef2[:, i : i + 1], scalar2=None, op0=MULT)
+
+        def store(k, u, j0, j1):
+            i = 2 * k + u
+            nc.sync.dma_start(out=out_v[:, i, JW * j0 : JW * j1], in_=res[i][:, JW * j0 : JW * j1])
+
+        for u in range(2):
+            for g in (1, 2):
+                transpose(0, g, u)
+        for u in range(2):
+            transpose(0, 0, u)
+        scale_out(0, 1, 0, 1)
+        scale_out(0, 2, 0, 1)
+        quant(0, 1, 0, 1)
+        scale_out(0, 1, 1, 2)
+        quant(0, 2, 0, 1)
+        scale_out(0, 2, 1, 2)
+        quant(0, 1, 1, 2)
+        scale_out(0, 0, 0, 1)
+        quant(0, 2, 1, 2)
+        scale_out(0, 0, 1, 2)
+        interleave_rd(0)
+        interleave_rd(1)
+        interleave_rd(2)
+        quant_rd(0)
+        quant(0, 0, 0, 2)
+        quant_rd(1)
+        for j in range(2):
+            for u in range(2):
+                mm(0, u, j, 1, True, False)
+                mm(0, u, j, 2, False, False)
+        for j in range(2):
+            for u in range(2):
+                mm(0, u, j, 0, False, True)
+                evac(0, u, j)
+        for u in range(2):
+            for g in (1, 2):
+                transpose(1, g, u)
+        for u in range(2):
+            transpose(1, 0, u)
+        quant_rd(2)
+        scale_out(1, 1, 0, 1)
+        scale_out(1, 2, 0, 1)
+        quant(1, 1, 0, 1)
+        scale_out(1, 0, 0, 1)
+        quant(1, 2, 0, 1)
+        scale_out(1, 1, 1, 2)
+        quant(1, 0, 0, 1)
+        scale_out(1, 2, 1, 2)
+        quant(1, 1, 1, 2)
+        scale_out(1, 0, 1, 2)
+        quant(1, 2, 1, 2)
+        quant(1, 0, 1, 2)
+        for u in range(2):
+            mm(0, u, 2, 1, True, False)
+            mm(0, u, 2, 2, False, False)
+        for u in range(2):
+            mm(0, u, 2, 0, False, True)
+            evac(0, u, 2)
+            store(0, u, 0, 3)
+            for what in PERM_AT.get((0, u), ()):
+                perm(*what)
+
+        def make_pair(k):
+            for g in (1, 2, 0):
+                for u in range(2):
+                    transpose(k, g, u)
+            scale_out(k, 1, 0, 2)
+            scale_out(k, 2, 0, 2)
+            quant(k, 1, 0, 2)
+            scale_out(k, 0, 0, 2)
+            quant(k, 2, 0, 2)
+            quant(k, 0, 0, 2)
+
+        for k in range(1, NPAIR):
+            last = k == NPAIR - 1
+            for n in range(6):
+                u, j = n // 3, n % 3
+                if not last and n == T_AT[k]:
+                    make_pair(k + 1)
+                mm(k, u, j, 1, True, False)
+                mm(k, u, j, 2, False, False)
+                mm(k, u, j, 0, False, True)
+                if last and n == 5:
+                    i = 2 * k + u
+                    for h, eng in ((0, nc.sync), (1, nc.scalar)):
+                        c0 = JW * j + 256 * h
+                        dst = res[i][:, c0 : c0 + 256]
+                        bank = acc[k, u, j][:, 256 * h : 256 * (h + 1)]
+                        if h == 0:
+                            nc.vector.tensor_scalar(out=dst, in0=bank, scalar1=ef2[:, i : i + 1], scalar2=None, op0=MULT)
+                        else:
+                            nc.scalar.activation(out=dst, in_=bank, func=COPY, scale=ef2[:, i : i + 1])
+                        eng.dma_start(out=out_v[:, i, c0 : c0 + 256], in_=dst)
+                    continue
+                evac(k, u, j, "v" if last and n % 2 == 0 else "s")
+                for what in PERM_AT.get((k, n), ()):
+                    perm(*what)
+                if last:
+                    store(k, u, j, j + 1)
+                elif j == 2:
+                    store(k, u, 0, 3)

@@ -11,269 +11,321 @@ U8 = mybir.dt.uint8
 FP8X4 = mybir.dt.float8_e4m3fn_x4
 FP4X4 = mybir.dt.float4_e2m1fn_x4
 MULT = mybir.AluOpType.mult
-ADD = mybir.AluOpType.add
 EXP = mybir.ActivationFunctionType.Exp
 COPY = mybir.ActivationFunctionType.Copy
 
 N = 1536
 FLOPS = 2 * N * N * N
 P = 128
-RT = N // P
-NPAIR = RT // 2
-NJ = 3
+TILES = N // P
+PAIRS = TILES // 2
 JW = 512
-S_COLS = 320
-T_AT = {1: 2, 2: 3, 3: 0, 4: 1}
-PERM_AT = {(0, 1): ((2, 0), (2, 1)), (1, 3): ((3, 0),), (1, 5): ((3, 1),), (2, 1): ((4, 0),), (2, 3): ((4, 1),), (3, 1): ((5, 0),), (3, 3): ((5, 1),)}
+JBLOCKS = N // JW
+BLOCKED = PAIRS - 1
+HALF = JW // 2
+QUARTER = JW // 4
 
 
 def tile_hubbard_slice_pair_s1_kernel(tc, left, f1, f2, r_d, r_p_words, r_p_scales, out):
     nc = tc.nc
-    left_v = left.rearrange("(p i) c -> p i c", i=RT)
-    out_v = out.rearrange("(p i) n -> p i n", i=RT)
-    rd_v = r_d.rearrange("(p j) w -> p j w", j=4)
-    rpw_v = r_p_words.rearrange("g p n -> p g n")
-    rps_v = r_p_scales.rearrange("g q n -> q g n")
+    left_rows = left.rearrange("(p i) c -> p i c", i=TILES)
+    left_cols = left.rearrange("(p i) (g q) -> p i g q", i=TILES, g=3)
+    out_rows = out.rearrange("(p i) n -> p i n", i=TILES)
+    rd_rows = r_d.rearrange("(p j) w -> p j w", j=4)
+    rp_rows = r_p_words.rearrange("g p n -> p g n")
+    rp_scale_rows = r_p_scales.rearrange("g q n -> q g n")
 
     with ExitStack() as ctx:
         keep = ctx.enter_context(tc.tile_pool(name="keep", bufs=1))
-        work = ctx.enter_context(tc.tile_pool(name="work", bufs=4))
+        work = ctx.enter_context(tc.tile_pool(name="work", bufs=2))
         psum = ctx.enter_context(tc.psum_pool(name="psum", bufs=8))
         ctx.enter_context(tc.manual_schedule())
 
         ident = keep.tile([P, P], F32, name="ident")
-        warm = keep.tile([P, 1], F32, name="warm")
-        f1_sb = keep.tile([P, 12], BF16, name="f1_sb")
-        f2_sb = keep.tile([P, 12], BF16, name="f2_sb")
-        ef1 = keep.tile([P, 12], F32, name="ef1")
-        ef2 = keep.tile([P, 12], F32, name="ef2")
-        rps = keep.tile([P, 2, N], U8, name="rps", align_bytes=64)
-        x_sb = [keep.tile([P, 2, N], BF16, name=f"x{k}", align_bytes=64) for k in range(NPAIR)]
-        rpw = [keep.tile([P, 2, 2 * JW], U8, name=f"rpw{j}", align_bytes=64) for j in range(NJ)]
-        rd_raw = [keep.tile([P, 4, JW], BF16, name=f"rdraw{j}", align_bytes=64) for j in range(NJ)]
-        rd_grp = [keep.tile([P, JW, 4], BF16, name=f"rdgrp{j}", align_bytes=64) for j in range(NJ)]
-        rdc = [keep.tile([P, JW], U32, name=f"rdc{j}", align_bytes=64) for j in range(NJ)]
-        rds = [keep.tile([P, JW], U8, name=f"rds{j}", align_bytes=64) for j in range(NJ)]
-        ac = [[keep.tile([P, 2 * P], U32, name=f"ac{k}_{g}", align_bytes=64) for g in range(3)] for k in range(NPAIR)]
-        asc = [[keep.tile([P, 2 * P], U8, name=f"as{k}_{g}", align_bytes=64) for g in range(3)] for k in range(NPAIR)]
+        zero = keep.tile([P, JW], BF16, name="zero", align_bytes=64)
+        zero_codes = keep.tile([P, P], U32, name="zero_codes", align_bytes=64)
+        zero_scales = keep.tile([P, P], U8, name="zero_scales", align_bytes=64)
+        table = keep.tile([P, 1], F32, name="table")
+        f1_raw = keep.tile([P, 3, 4], BF16, name="f1_raw")
+        f2_raw = keep.tile([P, TILES], BF16, name="f2_raw")
+        exp_f1 = keep.tile([P, 3, 4], F32, name="exp_f1")
+        exp_f2 = keep.tile([P, TILES], F32, name="exp_f2")
+        left0_p = [keep.tile([P, 2 * JW], BF16, name=f"left0_p{u}", align_bytes=64) for u in range(2)]
+        left0_d = keep.tile([P, 2, JW], BF16, name="left0_d", align_bytes=64)
+        left1 = [keep.tile([P, N], BF16, name=f"left1_{u}", align_bytes=64) for u in range(2)]
+        left_k = {k: keep.tile([P, 2, N], BF16, name=f"left{k}", align_bytes=64) for k in range(2, BLOCKED)}
+        left_b = keep.tile([P, 4, 2, 3, P], BF16, name="left_b", align_bytes=64)
+        rp_words = [keep.tile([P, 2, 2 * JW], U8, name=f"rp_words{j}", align_bytes=64) for j in range(JBLOCKS)]
+        rp_scales = keep.tile([P, 2, N], U8, name="rp_scales", align_bytes=64)
+        rd_raw = [keep.tile([P, 4, JW], BF16, name=f"rd_raw{j}", align_bytes=64) for j in range(JBLOCKS)]
+        rd_grouped = [keep.tile([P, JW, 4], BF16, name=f"rd_grouped{j}", align_bytes=64) for j in range(JBLOCKS)]
+        rd_codes = [keep.tile([P, JW], U32, name=f"rd_codes{j}", align_bytes=64) for j in range(JBLOCKS)]
+        rd_scales = [keep.tile([P, JW], U8, name=f"rd_scales{j}", align_bytes=64) for j in range(JBLOCKS)]
+        a_codes = [[keep.tile([P, 2 * P], U32, name=f"a_codes{k}_{g}", align_bytes=64) for g in range(3)] for k in range(PAIRS)]
+        a_scales = [[keep.tile([P, 2 * P], U8, name=f"a_scales{k}_{g}", align_bytes=64) for g in range(3)] for k in range(PAIRS)]
 
-        nc.vector.memset(warm[:], 0.0)
-        nc.vector.memset(rps[:].rearrange("p g n -> p (g n)").bitcast(I32), 0)
+        nc.vector.memset(table[:], 0.0)
+        nc.vector.memset(rp_scales[:].rearrange("p g n -> p (g n)").bitcast(I32), 0)
+        nc.vector.memset(zero[:].bitcast(I32), 0)
+        nc.vector.quantize_mx(out=zero_codes[:].bitcast(FP8X4), scales=zero_scales[:], in_=zero[:])
         make_identity(nc, ident[:])
-        nc.gpsimd.dma_start(out=f2_sb[:], in_=f2.rearrange("(p i) -> p i", i=RT))
+        nc.scalar.activation(out=table[:], in_=table[:], func=EXP)
+        nc.scalar.dma_start(out=f1_raw[:], in_=f1.rearrange("(g p t) -> p g t", p=P, t=4))
+        nc.scalar.dma_start(out=f2_raw[:], in_=f2.rearrange("(p i) -> p i", i=TILES))
+        nc.scalar.activation(out=exp_f1[:], in_=f1_raw[:], func=EXP)
 
-        nc.scalar.dma_start(out=f1_sb[:].rearrange("p (g t) -> p g t", t=4), in_=f1.rearrange("(g p t) -> p g t", p=P, t=4))
-        nc.scalar.activation(out=warm[:], in_=warm[:], func=EXP)
+        def load(dst, src):
+            nc.sync.dma_start(out=dst, in_=src)
 
-        def load_x(k, u0, u1, c0, c1):
-            nc.sync.dma_start(out=x_sb[k][:, u0:u1, c0:c1], in_=left_v[:, 2 * k + u0 : 2 * k + u1, c0:c1])
-
-        def load_rpw(j):
-            nc.sync.dma_start(out=rpw[j][:].bitcast(I32), in_=rpw_v[:, :, 2 * JW * j : 2 * JW * (j + 1)].bitcast(I32))
+        def load_rp(j):
+            load(rp_words[j][:].bitcast(I32), rp_rows[:, :, 2 * JW * j : 2 * JW * (j + 1)].bitcast(I32))
 
         def load_rd(j):
-            nc.sync.dma_start(out=rd_raw[j][:], in_=rd_v[:, :, JW * j : JW * (j + 1)])
+            load(rd_raw[j][:], rd_rows[:, :, JW * j : JW * (j + 1)])
 
-        load_x(0, 0, 1, 512, N)
-        load_x(0, 1, 2, 512, N)
-        load_rpw(0)
-        load_x(0, 0, 2, 0, 512)
-        for q in range(4):
-            nc.scalar.dma_start(out=rps[32 * q : 32 * q + 4, :, :].bitcast(I32), in_=rps_v[4 * q : 4 * q + 4, :, :].bitcast(I32))
+        def load_scales():
+            for q in range(4):
+                load(rp_scales[32 * q : 32 * q + 4].bitcast(I32), rp_scale_rows[4 * q : 4 * q + 4].bitcast(I32))
+
+        for u in range(2):
+            load(left0_p[u][:], left_rows[:, u, JW:])
+        load(left0_d[:], left_rows[:, 0:2, :JW])
+        load_scales()
         load_rd(0)
-        load_rpw(1)
+        load_rp(0)
+        load_rp(1)
+        load_rp(2)
         load_rd(1)
+        for u in range(2):
+            load(left1[u][:], left_rows[:, 2 + u])
         load_rd(2)
-        load_x(1, 0, 2, 512, N)
-        load_rpw(2)
-        load_x(1, 0, 2, 0, 512)
-        for k in range(2, NPAIR):
-            load_x(k, 0, 2, 0, N)
+        for k in range(2, BLOCKED):
+            load(left_k[k][:], left_rows[:, 2 * k : 2 * k + 2])
+        for a in range(4):
+            for b in range(4):
+                load(left_b[32 * a : 32 * a + 32, b], left_cols[32 * b : 32 * b + 32, 2 * BLOCKED : TILES, :, P * a : P * (a + 1)])
 
-        nc.scalar.activation(out=ef1[:], in_=f1_sb[:], func=EXP)
-        nc.scalar.activation(out=ef2[:], in_=f2_sb[:], func=EXP)
+        ordered, banks, grouped, open_groups, results = {}, {}, {}, {}, {}
 
-        tbank = {}
-        words = {}
+        def warm_up(n):
+            bank = psum.tile([P, JW], F32, name="bank")
+            for i in range(n):
+                nc.tensor.matmul_mx(out=bank[:, :P], lhsT=zero_codes[:].bitcast(FP8X4), lhsT_scale=zero_scales[:], rhs=zero_codes[:].bitcast(FP8X4), rhs_scale=zero_scales[:], start=True, stop=True)
 
-        def perm(k, u):
-            if (k, "perm") not in words:
-                pt = work.tile([P, 2, 3, 2, P], F32, name="perm", tag="perm", bufs=2)
-                words[k, "perm"] = pt
-            pt = words[k, "perm"]
-            src = x_sb[k][:, u, :].bitcast(F32)
-            nc.scalar.copy(out=pt[:, u], in_=src.rearrange("p (g m v) -> p g v m", g=3, v=2))
+        def order_words(k, u):
+            if k not in ordered:
+                pair_words = work.tile([P, 2, 3, 2, P], F32, name="pair_words", align_bytes=64, bufs=3)
+                ordered[k] = pair_words
+            nc.scalar.copy(out=ordered[k][:, u], in_=left_k[k][:, u].bitcast(F32).rearrange("p (g m v) -> p g v m", g=3, v=2))
+
+        def order_words_blocked(u):
+            tile_words = work.tile([P, 3, 2, 4, 32], F32, name="tile_words", align_bytes=64, bufs=2)
+            ordered[BLOCKED, u] = tile_words
+            src = left_b[:].rearrange("p b i g q -> p (b i g q)").bitcast(F32).rearrange("p (b i g m v) -> p i g v b m", b=4, i=2, g=3, v=2)
+            for g in range(3):
+                nc.scalar.copy(out=tile_words[:, g], in_=src[:, u, g])
+
+        def transpose_blocked(u):
+            turned = work.tile([P, 3 * HALF], F32, name="turned", align_bytes=64, bufs=2)
+            banks[BLOCKED, u] = turned
+            nc.vector.transpose(turned[:], ordered[BLOCKED, u][:].rearrange("p g v b m -> p (g v b m)"))
+
+        def words_of(k, g, u, v):
+            if k in ordered:
+                return ordered[k][:, u, g, v]
+            if k == 0:
+                row = left0_d[:, u] if g == 0 else left0_p[u][:, JW * (g - 1) : JW * g]
+            elif k == 1:
+                row = left1[u][:, JW * g : JW * (g + 1)]
+            else:
+                row = left_k[k][:, u, JW * g : JW * (g + 1)]
+            return row.bitcast(F32)[:, v:HALF:2]
+
+        def bank_place(k, g, u):
+            if k >= 2:
+                return (k, g), u
+            return ((k, 3 + u), g - 1) if g else ((k, 0), u)
 
         def transpose(k, g, u):
-            if (k, g) not in tbank:
-                bank = psum.tile([P, JW], F32, name="bank", tag="bank")
-                tbank[k, g] = bank
+            key, slot = bank_place(k, g, u)
+            if key not in banks:
+                bank = psum.tile([P, JW], F32, name="bank")
+                banks[key] = bank
             for v in range(2):
-                if (k, "perm") in words:
-                    src = words[k, "perm"][:, u, g, v, :]
+                at = HALF * v + P * slot
+                nc.tensor.transpose(banks[key][:, at : at + P], words_of(k, g, u, v), ident[:])
+
+        def scale(k, g, u, n=1):
+            if (k, g) not in grouped:
+                pair_grouped = work.tile([P, 2 * P, 4], BF16, name="pair_grouped", align_bytes=64, bufs=6)
+                grouped[k, g] = pair_grouped
+            if k == BLOCKED:
+                src, slot = banks[k, u][:, 2 * P * g : 2 * P * (g + 1)], 0
+            else:
+                key, slot = bank_place(k, g, u)
+                src = banks[key][:]
+            src = src.bitcast(BF16).rearrange("p (v r e) -> p r v e", v=2, e=2)[:, P * slot : P * (slot + n)]
+            factors = exp_f1[:, g].rearrange("p (v e) -> p v e", e=2).unsqueeze(1).to_broadcast([P, P * n, 2, 2])
+            dst = grouped[k, g][:, P * u : P * (u + n)].rearrange("p r (v e) -> p r v e", e=2)
+            nc.vector.tensor_tensor(out=dst, in0=src, in1=factors, op=MULT)
+
+        def quantize(k, g, u, n=1):
+            cols = slice(P * u, P * (u + n))
+            nc.vector.quantize_mx(out=a_codes[k][g][:, cols].bitcast(FP8X4), scales=a_scales[k][g][:, cols], in_=grouped[k, g][:, cols].rearrange("p r t -> p (r t)"))
+
+        def interleave(copy, j, quarter):
+            cols = slice(QUARTER * quarter, QUARTER * (quarter + 1))
+            copy(out=rd_grouped[j][:, cols], in_=rd_raw[j][:, :, cols].rearrange("p t w -> p w t"))
+
+        def quantize_rd(j):
+            nc.vector.quantize_mx(out=rd_codes[j][:].bitcast(FP8X4), scales=rd_scales[j][:], in_=rd_grouped[j][:].rearrange("p w t -> p (w t)"))
+
+        passes = {}
+
+        def multiply(k, u, j, *gs):
+            for g in gs:
+                if (k, u, j) not in open_groups:
+                    bank = psum.tile([P, JW], F32, name="bank")
+                    open_groups[k, u, j] = bank
+                done = passes.get((k, u, j), 0)
+                passes[k, u, j] = done + 1
+                if g == 0:
+                    rhs, rhs_scale = rd_codes[j][:].bitcast(FP8X4), rd_scales[j][:]
                 else:
-                    w = x_sb[k][:, u, :].bitcast(F32)
-                    src = w[:, 256 * g + v : 256 * (g + 1) : 2]
-                nc.tensor.transpose(tbank[k, g][:, 256 * v + P * u : 256 * v + P * (u + 1)], src, ident[:])
+                    rhs, rhs_scale = rp_words[j][:, g - 1].bitcast(FP4X4), rp_scales[:, g - 1, JW * j : JW * (j + 1)]
+                rows = slice(P * u, P * (u + 1))
+                nc.tensor.matmul_mx(out=open_groups[k, u, j][:], lhsT=a_codes[k][g][:, rows].bitcast(FP8X4), lhsT_scale=a_scales[k][g][:, rows], rhs=rhs, rhs_scale=rhs_scale, start=done == 0, stop=done == 2)
 
-        grp = {}
-
-        def scale_out(k, g, u0, u1):
-            if (k, g) not in grp:
-                gt = work.tile([P, 2 * P, 4], BF16, name="grp", tag="grp", align_bytes=64, bufs=6)
-                grp[k, g] = gt
-            n = P * (u1 - u0)
-            src = tbank[k, g][:].bitcast(BF16).rearrange("p (v x e) -> p x v e", v=2, e=2)[:, P * u0 : P * u1]
-            fac = ef1[:, 4 * g : 4 * g + 4].rearrange("p (v e) -> p v e", e=2).unsqueeze(1).to_broadcast([P, n, 2, 2])
-            dst = grp[k, g][:, P * u0 : P * u1, :].rearrange("p x (v e) -> p x v e", e=2)
-            nc.vector.tensor_tensor(out=dst, in0=src, in1=fac, op=MULT)
-
-        def quant(k, g, u0, u1):
-            nc.vector.quantize_mx(
-                out=ac[k][g][:, P * u0 : P * u1].bitcast(FP8X4),
-                scales=asc[k][g][:, P * u0 : P * u1],
-                in_=grp[k, g][:, P * u0 : P * u1, :].rearrange("p x t -> p (x t)"),
-            )
-
-        def interleave_rd(j):
-            nc.scalar.copy(out=rd_grp[j][:, :S_COLS, :], in_=rd_raw[j][:, :, :S_COLS].rearrange("p t w -> p w t"))
-            nc.gpsimd.tensor_scalar(
-                out=rd_grp[j][:, S_COLS:, :], in0=rd_raw[j][:, :, S_COLS:].rearrange("p t w -> p w t"),
-                scalar1=1.0, scalar2=0.0, op0=MULT, op1=ADD,
-            )
-
-        def quant_rd(j):
-            nc.vector.quantize_mx(out=rdc[j][:].bitcast(FP8X4), scales=rds[j][:], in_=rd_grp[j][:].rearrange("p w t -> p (w t)"))
-
-        acc = {}
-
-        def mm(k, u, j, g, start, stop):
-            if start:
-                bank = psum.tile([P, JW], F32, name="bank", tag="bank")
-                acc[k, u, j] = bank
-            if g == 0:
-                rhs = rdc[j][:].bitcast(FP8X4)
-                rhs_scale = rds[j][:]
-            else:
-                rhs = rpw[j][:, g - 1, :].bitcast(FP4X4)
-                rhs_scale = rps[:, g - 1, JW * j : JW * (j + 1)]
-            nc.tensor.matmul_mx(
-                out=acc[k, u, j][:],
-                lhsT=ac[k][g][:, P * u : P * (u + 1)].bitcast(FP8X4),
-                lhsT_scale=asc[k][g][:, P * u : P * (u + 1)],
-                rhs=rhs, rhs_scale=rhs_scale, start=start, stop=stop,
-            )
-
-        res = {}
-
-        def evac(k, u, j, engine="s"):
+        def finish(k, u, j, parts=1):
             i = 2 * k + u
-            if i not in res:
-                rt = work.tile([P, N], F32, name="res", tag="res", bufs=4)
-                res[i] = rt
-            dst = res[i][:, JW * j : JW * (j + 1)]
-            if engine == "s":
-                nc.scalar.activation(out=dst, in_=acc[k, u, j][:], func=COPY, scale=ef2[:, i : i + 1])
-            else:
-                nc.vector.tensor_scalar(out=dst, in0=acc[k, u, j][:], scalar1=ef2[:, i : i + 1], scalar2=None, op0=MULT)
+            if i not in results:
+                result = work.tile([P, N], F32, name="result", bufs=8)
+                results[i] = result
+            w = JW // parts
+            for h in range(parts):
+                cols = slice(JW * j + w * h, JW * j + w * (h + 1))
+                nc.scalar.activation(out=results[i][:, cols], in_=open_groups[k, u, j][:, w * h : w * (h + 1)], func=COPY, scale=exp_f2[:, i : i + 1])
+                if k == PAIRS - 1:
+                    nc.sync.dma_start(out=out_rows[:, i, cols], in_=results[i][:, cols])
+            if k < PAIRS - 1 and j == JBLOCKS - 1:
+                nc.sync.dma_start(out=out_rows[:, i], in_=results[i][:])
 
-        def store(k, u, j0, j1):
-            i = 2 * k + u
-            nc.sync.dma_start(out=out_v[:, i, JW * j0 : JW * j1], in_=res[i][:, JW * j0 : JW * j1])
-
+        on_s, on_v = nc.scalar.copy, nc.vector.tensor_copy
+        warm_up(14)
         for u in range(2):
-            for g in (1, 2):
-                transpose(0, g, u)
+            transpose(0, 1, u)
+            transpose(0, 2, u)
         for u in range(2):
             transpose(0, 0, u)
-        scale_out(0, 1, 0, 1)
-        scale_out(0, 2, 0, 1)
-        quant(0, 1, 0, 1)
-        scale_out(0, 1, 1, 2)
-        quant(0, 2, 0, 1)
-        scale_out(0, 2, 1, 2)
-        quant(0, 1, 1, 2)
-        scale_out(0, 0, 0, 1)
-        quant(0, 2, 1, 2)
-        scale_out(0, 0, 1, 2)
-        interleave_rd(0)
-        interleave_rd(1)
-        interleave_rd(2)
-        quant_rd(0)
-        quant(0, 0, 0, 2)
-        quant_rd(1)
-        for j in range(2):
+        warm_up(8)
+        for g in (1, 2):
+            scale(0, g, 0)
+        for g in (1, 2):
+            quantize(0, g, 0)
+        interleave(on_s, 0, 0)
+        interleave(on_s, 0, 1)
+        scale(0, 1, 1)
+        interleave(on_v, 0, 2)
+        quantize(0, 1, 1)
+        interleave(on_v, 0, 3)
+        scale(0, 2, 1)
+        quantize_rd(0)
+        quantize(0, 2, 1)
+        for u in range(2):
+            scale(0, 0, u)
+        for u in range(2):
+            quantize(0, 0, u)
+        for u in range(2):
+            for j in range(3):
+                multiply(0, u, j, 1, 2)
+        nc.scalar.activation(out=exp_f2[:], in_=f2_raw[:], func=EXP)
+        interleave(on_s, 1, 0)
+        interleave(on_s, 1, 1)
+        interleave(on_v, 1, 2)
+        interleave(on_v, 1, 3)
+        quantize_rd(1)
+        for u in range(2):
+            multiply(0, u, 0, 0)
+            finish(0, u, 0)
+        for g in (1, 2, 0):
+            transpose(1, g, 0)
+        for g in (1, 2, 0):
+            transpose(1, g, 1)
+        interleave(on_s, 2, 0)
+        interleave(on_s, 2, 1)
+        scale(1, 1, 0)
+        scale(1, 2, 0)
+        quantize(1, 1, 0)
+        quantize(1, 2, 0)
+        interleave(on_v, 2, 2)
+        interleave(on_v, 2, 3)
+        scale(1, 0, 0)
+        quantize_rd(2)
+        quantize(1, 0, 0)
+        scale(1, 1, 1)
+        scale(1, 2, 1)
+        quantize(1, 1, 1)
+        quantize(1, 2, 1)
+        scale(1, 0, 1)
+        for u in range(2):
+            multiply(0, u, 1, 0)
+            finish(0, u, 1)
+        for j in range(3):
+            multiply(1, 0, j, 1, 2)
+        for u in range(2):
+            multiply(0, u, 2, 0)
+            finish(0, u, 2)
+        multiply(1, 0, 0, 0)
+        finish(1, 0, 0)
+        for g in (1, 2, 0):
             for u in range(2):
-                mm(0, u, j, 1, True, False)
-                mm(0, u, j, 2, False, False)
-        for j in range(2):
-            for u in range(2):
-                mm(0, u, j, 0, False, True)
-                evac(0, u, j)
-        for u in range(2):
-            for g in (1, 2):
-                transpose(1, g, u)
-        for u in range(2):
-            transpose(1, 0, u)
-        quant_rd(2)
-        scale_out(1, 1, 0, 1)
-        scale_out(1, 2, 0, 1)
-        quant(1, 1, 0, 1)
-        scale_out(1, 0, 0, 1)
-        quant(1, 2, 0, 1)
-        scale_out(1, 1, 1, 2)
-        quant(1, 0, 0, 1)
-        scale_out(1, 2, 1, 2)
-        quant(1, 1, 1, 2)
-        scale_out(1, 0, 1, 2)
-        quant(1, 2, 1, 2)
-        quant(1, 0, 1, 2)
-        for u in range(2):
-            mm(0, u, 2, 1, True, False)
-            mm(0, u, 2, 2, False, False)
-        for u in range(2):
-            mm(0, u, 2, 0, False, True)
-            evac(0, u, 2)
-            store(0, u, 0, 3)
-            for what in PERM_AT.get((0, u), ()):
-                perm(*what)
-
-        def make_pair(k):
-            for g in (1, 2, 0):
+                transpose(2, g, u)
+        for j in (1, 2):
+            multiply(1, 0, j, 0)
+        order_words(3, 0)
+        order_words(3, 1)
+        for j in (1, 2):
+            finish(1, 0, j)
+        order_words(4, 0)
+        order_words(4, 1)
+        scale(2, 1, 0, 2)
+        quantize(1, 0, 1)
+        scale(2, 2, 0, 2)
+        quantize(2, 1, 0, 2)
+        scale(2, 0, 0, 2)
+        quantize(2, 2, 0, 2)
+        quantize(2, 0, 0, 2)
+        for j in range(3):
+            if j == 2:
+                for k in (3, 4):
+                    for g in (1, 2, 0):
+                        for u in range(2):
+                            transpose(k, g, u)
+            multiply(1, 1, j, 1, 2, 0)
+            finish(1, 1, j)
+        for k in (3, 4):
+            scale(k, 1, 0, 2)
+            scale(k, 2, 0, 2)
+            quantize(k, 1, 0, 2)
+            scale(k, 0, 0, 2)
+            quantize(k, 2, 0, 2)
+            quantize(k, 0, 0, 2)
+        for k in range(2, PAIRS):
+            if k == 2:
+                order_words_blocked(0)
+                order_words_blocked(1)
                 for u in range(2):
-                    transpose(k, g, u)
-            scale_out(k, 1, 0, 2)
-            scale_out(k, 2, 0, 2)
-            quant(k, 1, 0, 2)
-            scale_out(k, 0, 0, 2)
-            quant(k, 2, 0, 2)
-            quant(k, 0, 0, 2)
-
-        for k in range(1, NPAIR):
-            last = k == NPAIR - 1
-            for n in range(6):
-                u, j = n // 3, n % 3
-                if not last and n == T_AT[k]:
-                    make_pair(k + 1)
-                mm(k, u, j, 1, True, False)
-                mm(k, u, j, 2, False, False)
-                mm(k, u, j, 0, False, True)
-                if last and n == 5:
-                    i = 2 * k + u
-                    for h, eng in ((0, nc.sync), (1, nc.scalar)):
-                        c0 = JW * j + 256 * h
-                        dst = res[i][:, c0 : c0 + 256]
-                        bank = acc[k, u, j][:, 256 * h : 256 * (h + 1)]
-                        if h == 0:
-                            nc.vector.tensor_scalar(out=dst, in0=bank, scalar1=ef2[:, i : i + 1], scalar2=None, op0=MULT)
-                        else:
-                            nc.scalar.activation(out=dst, in_=bank, func=COPY, scale=ef2[:, i : i + 1])
-                        eng.dma_start(out=out_v[:, i, c0 : c0 + 256], in_=dst)
-                    continue
-                evac(k, u, j, "v" if last and n % 2 == 0 else "s")
-                for what in PERM_AT.get((k, n), ()):
-                    perm(*what)
-                if last:
-                    store(k, u, j, j + 1)
-                elif j == 2:
-                    store(k, u, 0, 3)
+                    transpose_blocked(u)
+                scale(5, 1, 0)
+                scale(5, 1, 1)
+                scale(5, 2, 0)
+                quantize(5, 1, 0, 2)
+                scale(5, 2, 1)
+                scale(5, 0, 0)
+                quantize(5, 2, 0, 2)
+                scale(5, 0, 1)
+                quantize(5, 0, 0, 2)
+            for u in range(2):
+                for j in range(3):
+                    multiply(k, u, j, 1, 2, 0)
+                    finish(k, u, j, 2 if (k, u, j) == (5, 1, 2) else 1)

from contextlib import ExitStack

import concourse.mybir as mybir
from concourse.masks import make_identity

F32 = mybir.dt.float32
BF16 = mybir.dt.bfloat16
I32 = mybir.dt.int32
U32 = mybir.dt.uint32
U8 = mybir.dt.uint8
FP8X4 = mybir.dt.float8_e4m3fn_x4
FP4X4 = mybir.dt.float4_e2m1fn_x4
MULT = mybir.AluOpType.mult
EXP = mybir.ActivationFunctionType.Exp
COPY = mybir.ActivationFunctionType.Copy

N = 1536
FLOPS = 2 * N * N * N
P = 128
TILES = N // P
PAIRS = TILES // 2
JW = 512
JBLOCKS = N // JW
BLOCKED = PAIRS - 1
HALF = JW // 2
QUARTER = JW // 4


def tile_hubbard_slice_pair_s1_kernel(tc, left, f1, f2, r_d, r_p_words, r_p_scales, out):
    nc = tc.nc
    left_rows = left.rearrange("(p i) c -> p i c", i=TILES)
    left_cols = left.rearrange("(p i) (g q) -> p i g q", i=TILES, g=3)
    out_rows = out.rearrange("(p i) n -> p i n", i=TILES)
    rd_rows = r_d.rearrange("(p j) w -> p j w", j=4)
    rp_rows = r_p_words.rearrange("g p n -> p g n")
    rp_scale_rows = r_p_scales.rearrange("g q n -> q g n")

    with ExitStack() as ctx:
        keep = ctx.enter_context(tc.tile_pool(name="keep", bufs=1))
        work = ctx.enter_context(tc.tile_pool(name="work", bufs=2))
        psum = ctx.enter_context(tc.psum_pool(name="psum", bufs=8))
        ctx.enter_context(tc.manual_schedule())

        ident = keep.tile([P, P], F32, name="ident")
        zero = keep.tile([P, JW], BF16, name="zero", align_bytes=64)
        zero_codes = keep.tile([P, P], U32, name="zero_codes", align_bytes=64)
        zero_scales = keep.tile([P, P], U8, name="zero_scales", align_bytes=64)
        table = keep.tile([P, 1], F32, name="table")
        f1_raw = keep.tile([P, 3, 4], BF16, name="f1_raw")
        f2_raw = keep.tile([P, TILES], BF16, name="f2_raw")
        exp_f1 = keep.tile([P, 3, 4], F32, name="exp_f1")
        exp_f2 = keep.tile([P, TILES], F32, name="exp_f2")
        left0_p = [keep.tile([P, 2 * JW], BF16, name=f"left0_p{u}", align_bytes=64) for u in range(2)]
        left0_d = keep.tile([P, 2, JW], BF16, name="left0_d", align_bytes=64)
        left1 = [keep.tile([P, N], BF16, name=f"left1_{u}", align_bytes=64) for u in range(2)]
        left_k = {k: keep.tile([P, 2, N], BF16, name=f"left{k}", align_bytes=64) for k in range(2, BLOCKED)}
        left_b = keep.tile([P, 4, 2, 3, P], BF16, name="left_b", align_bytes=64)
        rp_words = [keep.tile([P, 2, 2 * JW], U8, name=f"rp_words{j}", align_bytes=64) for j in range(JBLOCKS)]
        rp_scales = keep.tile([P, 2, N], U8, name="rp_scales", align_bytes=64)
        rd_raw = [keep.tile([P, 4, JW], BF16, name=f"rd_raw{j}", align_bytes=64) for j in range(JBLOCKS)]
        rd_grouped = [keep.tile([P, JW, 4], BF16, name=f"rd_grouped{j}", align_bytes=64) for j in range(JBLOCKS)]
        rd_codes = [keep.tile([P, JW], U32, name=f"rd_codes{j}", align_bytes=64) for j in range(JBLOCKS)]
        rd_scales = [keep.tile([P, JW], U8, name=f"rd_scales{j}", align_bytes=64) for j in range(JBLOCKS)]
        a_codes = [[keep.tile([P, 2 * P], U32, name=f"a_codes{k}_{g}", align_bytes=64) for g in range(3)] for k in range(PAIRS)]
        a_scales = [[keep.tile([P, 2 * P], U8, name=f"a_scales{k}_{g}", align_bytes=64) for g in range(3)] for k in range(PAIRS)]

        nc.vector.memset(table[:], 0.0)
        nc.vector.memset(rp_scales[:].rearrange("p g n -> p (g n)").bitcast(I32), 0)
        nc.vector.memset(zero[:].bitcast(I32), 0)
        nc.vector.quantize_mx(out=zero_codes[:].bitcast(FP8X4), scales=zero_scales[:], in_=zero[:])
        make_identity(nc, ident[:])
        nc.scalar.activation(out=table[:], in_=table[:], func=EXP)
        nc.scalar.dma_start(out=f1_raw[:], in_=f1.rearrange("(g p t) -> p g t", p=P, t=4))
        nc.scalar.dma_start(out=f2_raw[:], in_=f2.rearrange("(p i) -> p i", i=TILES))
        nc.scalar.activation(out=exp_f1[:], in_=f1_raw[:], func=EXP)

        def load(dst, src):
            nc.sync.dma_start(out=dst, in_=src)

        def load_rp(j):
            load(rp_words[j][:].bitcast(I32), rp_rows[:, :, 2 * JW * j : 2 * JW * (j + 1)].bitcast(I32))

        def load_rd(j):
            load(rd_raw[j][:], rd_rows[:, :, JW * j : JW * (j + 1)])

        def load_scales():
            for q in range(4):
                load(rp_scales[32 * q : 32 * q + 4].bitcast(I32), rp_scale_rows[4 * q : 4 * q + 4].bitcast(I32))

        for u in range(2):
            load(left0_p[u][:], left_rows[:, u, JW:])
        load(left0_d[:], left_rows[:, 0:2, :JW])
        load_scales()
        load_rd(0)
        load_rp(0)
        load_rp(1)
        load_rp(2)
        load_rd(1)
        for u in range(2):
            load(left1[u][:], left_rows[:, 2 + u])
        load_rd(2)
        for k in range(2, BLOCKED):
            load(left_k[k][:], left_rows[:, 2 * k : 2 * k + 2])
        for a in range(4):
            for b in range(4):
                load(left_b[32 * a : 32 * a + 32, b], left_cols[32 * b : 32 * b + 32, 2 * BLOCKED : TILES, :, P * a : P * (a + 1)])

        ordered, banks, grouped, open_groups, results = {}, {}, {}, {}, {}

        def warm_up(n):
            bank = psum.tile([P, JW], F32, name="bank")
            for i in range(n):
                nc.tensor.matmul_mx(out=bank[:, :P], lhsT=zero_codes[:].bitcast(FP8X4), lhsT_scale=zero_scales[:], rhs=zero_codes[:].bitcast(FP8X4), rhs_scale=zero_scales[:], start=True, stop=True)

        def order_words(k, u):
            if k not in ordered:
                pair_words = work.tile([P, 2, 3, 2, P], F32, name="pair_words", align_bytes=64, bufs=3)
                ordered[k] = pair_words
            nc.scalar.copy(out=ordered[k][:, u], in_=left_k[k][:, u].bitcast(F32).rearrange("p (g m v) -> p g v m", g=3, v=2))

        def order_words_blocked(u):
            tile_words = work.tile([P, 3, 2, 4, 32], F32, name="tile_words", align_bytes=64, bufs=2)
            ordered[BLOCKED, u] = tile_words
            src = left_b[:].rearrange("p b i g q -> p (b i g q)").bitcast(F32).rearrange("p (b i g m v) -> p i g v b m", b=4, i=2, g=3, v=2)
            for g in range(3):
                nc.scalar.copy(out=tile_words[:, g], in_=src[:, u, g])

        def transpose_blocked(u):
            turned = work.tile([P, 3 * HALF], F32, name="turned", align_bytes=64, bufs=2)
            banks[BLOCKED, u] = turned
            nc.vector.transpose(turned[:], ordered[BLOCKED, u][:].rearrange("p g v b m -> p (g v b m)"))

        def words_of(k, g, u, v):
            if k in ordered:
                return ordered[k][:, u, g, v]
            if k == 0:
                row = left0_d[:, u] if g == 0 else left0_p[u][:, JW * (g - 1) : JW * g]
            elif k == 1:
                row = left1[u][:, JW * g : JW * (g + 1)]
            else:
                row = left_k[k][:, u, JW * g : JW * (g + 1)]
            return row.bitcast(F32)[:, v:HALF:2]

        def bank_place(k, g, u):
            if k >= 2:
                return (k, g), u
            return ((k, 3 + u), g - 1) if g else ((k, 0), u)

        def transpose(k, g, u):
            key, slot = bank_place(k, g, u)
            if key not in banks:
                bank = psum.tile([P, JW], F32, name="bank")
                banks[key] = bank
            for v in range(2):
                at = HALF * v + P * slot
                nc.tensor.transpose(banks[key][:, at : at + P], words_of(k, g, u, v), ident[:])

        def scale(k, g, u, n=1):
            if (k, g) not in grouped:
                pair_grouped = work.tile([P, 2 * P, 4], BF16, name="pair_grouped", align_bytes=64, bufs=6)
                grouped[k, g] = pair_grouped
            if k == BLOCKED:
                src, slot = banks[k, u][:, 2 * P * g : 2 * P * (g + 1)], 0
            else:
                key, slot = bank_place(k, g, u)
                src = banks[key][:]
            src = src.bitcast(BF16).rearrange("p (v r e) -> p r v e", v=2, e=2)[:, P * slot : P * (slot + n)]
            factors = exp_f1[:, g].rearrange("p (v e) -> p v e", e=2).unsqueeze(1).to_broadcast([P, P * n, 2, 2])
            dst = grouped[k, g][:, P * u : P * (u + n)].rearrange("p r (v e) -> p r v e", e=2)
            nc.vector.tensor_tensor(out=dst, in0=src, in1=factors, op=MULT)

        def quantize(k, g, u, n=1):
            cols = slice(P * u, P * (u + n))
            nc.vector.quantize_mx(out=a_codes[k][g][:, cols].bitcast(FP8X4), scales=a_scales[k][g][:, cols], in_=grouped[k, g][:, cols].rearrange("p r t -> p (r t)"))

        def interleave(copy, j, quarter):
            cols = slice(QUARTER * quarter, QUARTER * (quarter + 1))
            copy(out=rd_grouped[j][:, cols], in_=rd_raw[j][:, :, cols].rearrange("p t w -> p w t"))

        def quantize_rd(j):
            nc.vector.quantize_mx(out=rd_codes[j][:].bitcast(FP8X4), scales=rd_scales[j][:], in_=rd_grouped[j][:].rearrange("p w t -> p (w t)"))

        passes = {}

        def multiply(k, u, j, *gs):
            for g in gs:
                if (k, u, j) not in open_groups:
                    bank = psum.tile([P, JW], F32, name="bank")
                    open_groups[k, u, j] = bank
                done = passes.get((k, u, j), 0)
                passes[k, u, j] = done + 1
                if g == 0:
                    rhs, rhs_scale = rd_codes[j][:].bitcast(FP8X4), rd_scales[j][:]
                else:
                    rhs, rhs_scale = rp_words[j][:, g - 1].bitcast(FP4X4), rp_scales[:, g - 1, JW * j : JW * (j + 1)]
                rows = slice(P * u, P * (u + 1))
                nc.tensor.matmul_mx(out=open_groups[k, u, j][:], lhsT=a_codes[k][g][:, rows].bitcast(FP8X4), lhsT_scale=a_scales[k][g][:, rows], rhs=rhs, rhs_scale=rhs_scale, start=done == 0, stop=done == 2)

        def finish(k, u, j, parts=1):
            i = 2 * k + u
            if i not in results:
                result = work.tile([P, N], F32, name="result", bufs=8)
                results[i] = result
            w = JW // parts
            for h in range(parts):
                cols = slice(JW * j + w * h, JW * j + w * (h + 1))
                nc.scalar.activation(out=results[i][:, cols], in_=open_groups[k, u, j][:, w * h : w * (h + 1)], func=COPY, scale=exp_f2[:, i : i + 1])
                if k == PAIRS - 1:
                    nc.sync.dma_start(out=out_rows[:, i, cols], in_=results[i][:, cols])
            if k < PAIRS - 1 and j == JBLOCKS - 1:
                nc.sync.dma_start(out=out_rows[:, i], in_=results[i][:])

        on_s, on_v = nc.scalar.copy, nc.vector.tensor_copy
        warm_up(14)
        for u in range(2):
            transpose(0, 1, u)
            transpose(0, 2, u)
        for u in range(2):
            transpose(0, 0, u)
        warm_up(8)
        for g in (1, 2):
            scale(0, g, 0)
        for g in (1, 2):
            quantize(0, g, 0)
        interleave(on_s, 0, 0)
        interleave(on_s, 0, 1)
        scale(0, 1, 1)
        interleave(on_v, 0, 2)
        quantize(0, 1, 1)
        interleave(on_v, 0, 3)
        scale(0, 2, 1)
        quantize_rd(0)
        quantize(0, 2, 1)
        for u in range(2):
            scale(0, 0, u)
        for u in range(2):
            quantize(0, 0, u)
        for u in range(2):
            for j in range(3):
                multiply(0, u, j, 1, 2)
        nc.scalar.activation(out=exp_f2[:], in_=f2_raw[:], func=EXP)
        interleave(on_s, 1, 0)
        interleave(on_s, 1, 1)
        interleave(on_v, 1, 2)
        interleave(on_v, 1, 3)
        quantize_rd(1)
        for u in range(2):
            multiply(0, u, 0, 0)
            finish(0, u, 0)
        for g in (1, 2, 0):
            transpose(1, g, 0)
        for g in (1, 2, 0):
            transpose(1, g, 1)
        interleave(on_s, 2, 0)
        interleave(on_s, 2, 1)
        scale(1, 1, 0)
        scale(1, 2, 0)
        quantize(1, 1, 0)
        quantize(1, 2, 0)
        interleave(on_v, 2, 2)
        interleave(on_v, 2, 3)
        scale(1, 0, 0)
        quantize_rd(2)
        quantize(1, 0, 0)
        scale(1, 1, 1)
        scale(1, 2, 1)
        quantize(1, 1, 1)
        quantize(1, 2, 1)
        scale(1, 0, 1)
        for u in range(2):
            multiply(0, u, 1, 0)
            finish(0, u, 1)
        for j in range(3):
            multiply(1, 0, j, 1, 2)
        for u in range(2):
            multiply(0, u, 2, 0)
            finish(0, u, 2)
        multiply(1, 0, 0, 0)
        finish(1, 0, 0)
        for g in (1, 2, 0):
            for u in range(2):
                transpose(2, g, u)
        for j in (1, 2):
            multiply(1, 0, j, 0)
        order_words(3, 0)
        order_words(3, 1)
        for j in (1, 2):
            finish(1, 0, j)
        order_words(4, 0)
        order_words(4, 1)
        scale(2, 1, 0, 2)
        quantize(1, 0, 1)
        scale(2, 2, 0, 2)
        quantize(2, 1, 0, 2)
        scale(2, 0, 0, 2)
        quantize(2, 2, 0, 2)
        quantize(2, 0, 0, 2)
        for j in range(3):
            if j == 2:
                for k in (3, 4):
                    for g in (1, 2, 0):
                        for u in range(2):
                            transpose(k, g, u)
            multiply(1, 1, j, 1, 2, 0)
            finish(1, 1, j)
        for k in (3, 4):
            scale(k, 1, 0, 2)
            scale(k, 2, 0, 2)
            quantize(k, 1, 0, 2)
            scale(k, 0, 0, 2)
            quantize(k, 2, 0, 2)
            quantize(k, 0, 0, 2)
        for k in range(2, PAIRS):
            if k == 2:
                order_words_blocked(0)
                order_words_blocked(1)
                for u in range(2):
                    transpose_blocked(u)
                scale(5, 1, 0)
                scale(5, 1, 1)
                scale(5, 2, 0)
                quantize(5, 1, 0, 2)
                scale(5, 2, 1)
                scale(5, 0, 0)
                quantize(5, 2, 0, 2)
                scale(5, 0, 1)
                quantize(5, 0, 0, 2)
            for u in range(2):
                for j in range(3):
                    multiply(k, u, j, 1, 2, 0)
                    finish(k, u, j, 2 if (k, u, j) == (5, 1, 2) else 1)
